import numpy as np
import ml_dtypes


def mxq(x, axis, fmt="e4m3"):
    dtype, down = {"e4m3": (ml_dtypes.float8_e4m3fn, 7), "e5m2": (ml_dtypes.float8_e5m2, 14)}[fmt]
    v = np.moveaxis(np.asarray(x, np.float32).astype(ml_dtypes.bfloat16).astype(np.float64), axis, -1)
    blocks = v.reshape(v.shape[:-1] + (-1, 32))
    amax = np.abs(blocks).max(-1, keepdims=True)
    byte = np.maximum(np.where(amax > 0, np.frexp(amax)[1] - 1 + 127, 0) - down, 1)
    scale = np.exp2(byte - 127.0)
    codes = (blocks / scale).astype(np.float32).astype(dtype).astype(np.float64)
    return np.moveaxis((codes * scale).reshape(v.shape), -1, axis)


WIDE = False


def mx_kscale(k):
    if not WIDE:
        return np.ones(k)
    levels = np.array([30, -30])
    if k % 512:
        return np.exp2(np.random.permutation(np.resize(levels, k // 32))).repeat(32)
    a = np.empty((k // 512, 16))
    for p in range(k // 512):
        a[p, :8] = np.random.permutation(np.resize(levels, 8))
        for g in range(8):
            far = levels[np.abs(levels - a[p, g]) >= 10]
            a[p, g + 8] = far[np.random.randint(len(far))]
    return np.exp2(a.ravel()).repeat(32)


BF16 = ml_dtypes.bfloat16


def bf(x):
    return np.asarray(x, np.float32).astype(BF16)


def f64(x):
    return np.asarray(x).astype(np.float64)


E2M1 = np.array([0.0, 0.5, 1.0, 1.5, 2.0, 3.0, 4.0, 6.0, -0.0, -0.5, -1.0, -1.5, -2.0, -3.0, -4.0, -6.0])


def pack_weight(w, fmt):
    k, n = w.shape
    w = f64(bf(w)).reshape(k // 32, 32, n)
    amax = np.abs(w).max(1)
    if fmt == "e4m3":
        byte = np.frexp(amax)[1] - 1 + 127 - 7
    else:
        mant, ex = np.frexp(amax / 6.0)
        byte = np.where(mant > 0.5, ex, ex - 1) + 127
    byte = np.clip(np.where(amax > 0, byte, 1), 1, 254)
    scaled = (w * np.exp2(127.0 - byte)[:, None, :]).reshape(k, n).astype(np.float32)
    by_word = np.ascontiguousarray(scaled.reshape(k // 512, 128, 4, n).transpose(0, 1, 3, 2))
    if fmt == "e4m3":
        words = by_word.astype(ml_dtypes.float8_e4m3fn).view(np.uint8)
    else:
        c = by_word.astype(ml_dtypes.float4_e2m1fn).view(np.uint8) & 0xF
        words = c[..., 0::2] | (c[..., 1::2] << 4)
    return np.ascontiguousarray(words), np.ascontiguousarray(byte.astype(np.uint8).reshape(k // 512, 16, n))


def unpack_weight(words, scales, fmt):
    g, p, n, _ = words.shape
    if fmt == "e4m3":
        vals = np.ascontiguousarray(words).view(ml_dtypes.float8_e4m3fn).astype(np.float64)
    else:
        nib = np.empty((g, p, n, 4), np.uint8)
        nib[..., 0::2] = words & 0xF
        nib[..., 1::2] = words >> 4
        vals = E2M1[nib]
    vals = vals * np.repeat(np.exp2(scales.astype(np.float64) - 127.0), 8, axis=1)[..., None]
    return vals.transpose(0, 1, 3, 2).reshape(g * 512, n)
def pack4(w):
    words, scales = pack_weight(w, "e2m1")
    return words.reshape(words.shape[0], 128, -1), scales


def unpack4(words, scales):
    return unpack_weight(words.reshape(words.shape[0], 128, -1, 2), scales, "e2m1")


M, D, F = 1024, 1024, 1536


def setup_inputs():
    s, t = mx_kscale(D), mx_kscale(F)
    head = np.random.standard_normal((D, F)) / np.sqrt(D)
    w_words, w_scales = pack4(head / s[:, None])
    return {"x": bf(np.random.standard_normal((M, D)) * s),
            "w_words": w_words,
            "w_scales": w_scales,
            "y": bf(np.random.standard_normal((M, F))),
            "c": bf((1 + 0.1 * np.random.standard_normal(F)) * t),
            "v": bf(head.T / t[:, None])}


def reference(x, w_words, w_scales, y, c, v):
    pred = mxq(f64(x), 1, "e4m3") @ unpack4(w_words, w_scales)
    e = np.tanh(pred - f64(y)) * f64(c)
    dx = mxq(e, 1, "e5m2") @ mxq(f64(v), 0, "e4m3")
    return dx

@@ -1,0 +1,352 @@
+from contextlib import ExitStack
+
+import concourse.mybir as mybir
+from concourse.masks import make_identity
+
+M, D, F = 1024, 1024, 1536
+FLOPS = 2 * M * D * F * 2
+
+F32 = mybir.dt.float32
+BF16 = mybir.dt.bfloat16
+I32 = mybir.dt.int32
+U32 = mybir.dt.uint32
+U8 = mybir.dt.uint8
+E4 = mybir.dt.float8_e4m3fn_x4
+E5 = mybir.dt.float8_e5m2_x4
+E2 = mybir.dt.float4_e2m1fn_x4
+ALU = mybir.AluOpType
+ACT = mybir.ActivationFunctionType
+
+P = 128
+N = 512
+TILES = M // P
+XG = D // N
+FG = F // N
+HALVES = D // N
+
+MODES = "TTTTMMMT"
+X_STEP = [0, 0, 0, 1, 1, 2, 2, 3]
+XQ_STEP = [0, 0, 0, 1, 2, 3, 4, 5]
+V_ENG = "VGSGSG"
+V_STEP = [0, 1, 1, 2, 2, 3]
+VQ_STEP = [1, 1, 2, 2, 3, 3]
+V_BUFS = {"V": 3, "S": 4, "G": 1}
+S2_COUNT = [0, 0, 0, 2, 3, 3, 2, 2, 2]
+SHARE = [[0, 0, 0], [0, 0, 1], [0, 0, 1], [1, 1, 1], [0, 1, 1], [0, 2, 1], [0, 1, 1], [0, 1, 0], [0, 2, 1]]
+LOAD_ORDER = "x0 x1 c w0 s y0a w1 y0b x2 v0 y1 v1 x3 x4 v2 y2 v3 x5 x6 x7 v4 y3 v5 y4 y5 y6 y7"
+
+
+def tile_data2vec_head_backward_s9_kernel(tc, x, w_words, w_scales, y, c, v, out):
+    nc = tc.nc
+    with ExitStack() as ctx:
+        keep = ctx.enter_context(tc.tile_pool(name="keep", bufs=1))
+        work = ctx.enter_context(tc.tile_pool(name="work", bufs=2))
+        psum = ctx.enter_context(tc.psum_pool(name="psum", bufs=1))
+        ctx.enter_context(tc.manual_schedule())
+
+        x_raw = [keep.tile([P, D], BF16, name="x_raw%d" % m, align_bytes=64) for m in range(TILES)]
+        y_raw = [keep.tile([P, F], BF16, name="y_raw%d" % m, align_bytes=64) for m in range(1, TILES)]
+        y_first = keep.tile([P, N], BF16, name="y_first", align_bytes=64)
+        y_rest = keep.tile([P, F - N], BF16, name="y_rest", align_bytes=64)
+        w_first = keep.tile([P, XG, 2 * N], U8, name="w_first", align_bytes=64)
+        w_rest = keep.tile([P, XG, 2 * (F - N)], U8, name="w_rest", align_bytes=64)
+        w_plane = keep.tile([P, XG, F], U8, name="w_plane", align_bytes=64)
+        v_raw = [keep.tile([P, 4, N], BF16, name="v_raw%d" % i, align_bytes=64) for i in range(HALVES * FG)]
+        c_col = keep.tile([P, FG, 16], BF16, name="c_col", align_bytes=64)
+        c_row = keep.tile([P, 2 * N], BF16, name="c_row", align_bytes=64)
+        ident = keep.tile([P, P], F32, name="ident", align_bytes=64)
+        warm = keep.tile([P, 16], F32, name="warm", align_bytes=64)
+
+        def y_cols(m, g):
+            if m > 0:
+                return y_raw[m - 1][:, g * N : (g + 1) * N]
+            return y_first[:] if g == 0 else y_rest[:, (g - 1) * N : g * N]
+
+        def w_cols(kg, g):
+            if g == 0:
+                return w_first[:, kg, :]
+            return w_rest[:, kg, (g - 1) * 2 * N : g * 2 * N]
+
+        nc.vector.memset(w_plane[:].rearrange("p g n -> p (g n)").bitcast(I32), 0)
+        nc.vector.memset(warm[:, 0:1], 0.0)
+        make_identity(nc, ident[:])
+        nc.scalar.activation(out=warm[:, 8:9], in_=warm[:, 0:1], func=ACT.Tanh)
+
+        w_i32 = w_words.bitcast(I32).rearrange("g p n -> p g n")
+        s_i32 = w_scales.bitcast(I32).rearrange("g q n -> q g n")
+        for item in LOAD_ORDER.split(" "):
+            if item == "w0":
+                nc.sync.dma_start(out=w_first[:].bitcast(I32), in_=w_i32[:, :, 0 : N // 2])
+            elif item == "w1":
+                nc.sync.dma_start(out=w_rest[:].bitcast(I32), in_=w_i32[:, :, N // 2 : F // 2])
+            elif item == "s":
+                for q in range(4):
+                    nc.sync.dma_start(out=w_plane[32 * q : 32 * q + 4].bitcast(I32), in_=s_i32[4 * q : 4 * q + 4])
+            elif item == "y0a":
+                nc.sync.dma_start(out=y_first[:], in_=y[0:P, 0:N])
+            elif item == "y0b":
+                nc.sync.dma_start(out=y_rest[:], in_=y[0:P, N:F])
+            elif item == "c":
+                nc.sync.dma_start(out=c_col[:, :, 0:4], in_=c.rearrange("(g p t) -> p g t", p=P, t=4))
+            elif item.startswith("x"):
+                m = int(item[1:])
+                nc.sync.dma_start(out=x_raw[m][:], in_=x[m * P : (m + 1) * P, :])
+            elif item.startswith("y"):
+                m = int(item[1:])
+                nc.sync.dma_start(out=y_raw[m - 1][:], in_=y[m * P : (m + 1) * P, :])
+            else:
+                i = int(item[1:])
+                h, g = divmod(i, FG)
+                nc.sync.dma_start(
+                    out=v_raw[i][:],
+                    in_=v[g * N : (g + 1) * N, h * N : (h + 1) * N].rearrange("(p t) n -> p t n", t=4),
+                )
+
+        x_bank, x_grp, x_codes, x_scales = {}, {}, {}, {}
+        pred, diff, th, e_rows, e_bank, e_grp, e_codes, e_scales = {}, {}, {}, {}, {}, {}, {}, {}
+        v_grp, v_codes, v_scales, o_bank = {}, {}, {}, {}
+
+        def x_transpose(m):
+            x_bank[m] = psum.tile([P, XG, 2, P], F32, name="xo_bank", bufs=2)
+            words = x_raw[m][:].bitcast(F32)
+            for g in range(XG):
+                for u in range(2):
+                    nc.tensor.transpose(x_bank[m][:, g, u, :], words[:, 256 * g + u : 256 * (g + 1) : 2], ident[:])
+
+        def x_copy(m):
+            x_grp[m] = work.tile([P, D], BF16, name="x_grp", bufs=TILES, align_bytes=64)
+            nc.scalar.copy(
+                out=x_grp[m][:].bitcast(F32).rearrange("p (g r u) -> p g r u", g=XG, u=2),
+                in_=x_bank[m][:].rearrange("p g u r -> p g r u"),
+            )
+
+        def x_quant(m):
+            x_codes[m] = work.tile([P, D // 4], U32, name="x_codes", bufs=3, align_bytes=64)
+            x_scales[m] = work.tile([P, D // 4], U8, name="x_scales", bufs=3, align_bytes=64)
+            nc.vector.quantize_mx(out=x_codes[m][:].bitcast(E4), scales=x_scales[m][:], in_=x_grp[m][:])
+
+        def c_spread():
+            words = c_col[:].bitcast(F32)
+            bank = psum.tile([P, 4, P], F32, name="e_bank", bufs=3)
+            for g in range(2):
+                for u in range(2):
+                    nc.tensor.transpose(bank[:, 2 * g + u, :], words[:, g, u : u + 1].to_broadcast([P, P]), ident[:])
+            nc.scalar.copy(out=c_row[:].bitcast(F32), in_=bank[:].rearrange("p a r -> p (a r)"))
+
+        def first_product(m):
+            for g in range(FG):
+                pred[m, g] = psum.tile([P, N], F32, name="pred", bufs=3)
+                for kg in range(XG):
+                    nc.tensor.matmul_mx(
+                        out=pred[m, g][:],
+                        lhsT=x_codes[m][:, kg * P : (kg + 1) * P].bitcast(E4),
+                        lhsT_scale=x_scales[m][:, kg * P : (kg + 1) * P],
+                        rhs=w_cols(kg, g).bitcast(E2),
+                        rhs_scale=w_plane[:, kg, g * N : (g + 1) * N],
+                        start=(kg == 0),
+                        stop=(kg == XG - 1),
+                    )
+
+        def subtract(m, g):
+            diff[m, g] = work.tile([P, N], F32, name="diff", bufs=3, align_bytes=64)
+            u, e = (4, 1) if MODES[m] == "T" or g == FG - 1 else (2, 2)
+            nc.vector.tensor_tensor(
+                out=diff[m, g][:].rearrange("p (u q e) -> p u q e", u=u, e=e),
+                in0=pred[m, g][:].rearrange("p (q u e) -> p u q e", u=u, e=e),
+                in1=y_cols(m, g).rearrange("p (q u e) -> p u q e", u=u, e=e),
+                op=ALU.subtract,
+            )
+
+        def tanh(m, g):
+            th[m, g] = work.tile([P, N], F32, name="th", bufs=4, align_bytes=64)
+            nc.scalar.activation(out=th[m, g][:], in_=diff[m, g][:], func=ACT.Tanh)
+
+        def weigh(m, g):
+            e_rows[m, g] = work.tile([P, N], BF16, name="e_rows", bufs=6, align_bytes=64)
+            nc.vector.tensor_tensor(
+                out=e_rows[m, g][:], in0=th[m, g][:], in1=c_row[:, g * N : (g + 1) * N], op=ALU.mult
+            )
+
+        def e_transpose(m):
+            e_bank[m, 0] = psum.tile([P, 2, 2, P], F32, name="e_bank", bufs=3)
+            for g in range(2):
+                words = e_rows[m, g][:].bitcast(F32)
+                for u in range(2):
+                    nc.tensor.transpose(e_bank[m, 0][:, g, u, :], words[:, u * P : (u + 1) * P], ident[:])
+
+        def th_transpose(m, g):
+            e_bank[m, g] = psum.tile([P, 4, P], F32, name="pred" if m == TILES - 1 else "e_bank", bufs=3)
+            for t in range(4):
+                nc.tensor.transpose(e_bank[m, g][:, t, :], th[m, g][:, t * P : (t + 1) * P], ident[:])
+
+        def pieces(m):
+            return ((0, 1), (1, 2), (2, 3)) if m == TILES - 1 else ((0, 2), (2, 3))
+
+        def piece_of(m, g):
+            return [(g0, g1) for g0, g1 in pieces(m) if g0 <= g < g1][0]
+
+        def weigh_turned(m, g):
+            g0, g1 = piece_of(m, g)
+            if g == g0:
+                e_grp[m, g0] = work.tile([P, (g1 - g0) * N], BF16, name="e_grp%d" % g0, bufs=2, align_bytes=64)
+            nc.vector.tensor_tensor(
+                out=e_grp[m, g0][:, (g - g0) * N : (g - g0 + 1) * N].rearrange("p (r t) -> p r t", t=4),
+                in0=e_bank[m, g][:].rearrange("p t r -> p r t"),
+                in1=c_col[:, g : g + 1, 0:4].to_broadcast([P, P, 4]),
+                op=ALU.mult,
+            )
+
+        def e_copy(m, g0, g1):
+            e_grp[m, g0] = work.tile([P, (g1 - g0) * N], BF16, name="e_grp%d" % g0, bufs=2, align_bytes=64)
+            nc.scalar.copy(
+                out=e_grp[m, g0][:].bitcast(F32).rearrange("p (g r u) -> p g r u", r=P, u=2),
+                in_=e_bank[m, g0][:, 0 : g1 - g0].rearrange("p g u r -> p g r u"),
+            )
+
+        def e_quant(m, g0, g1):
+            e_codes[m, g0] = keep.tile([P, (g1 - g0) * P], U32, name="e_codes%d_%d" % (m, g0), align_bytes=64)
+            e_scales[m, g0] = keep.tile([P, (g1 - g0) * P], U8, name="e_scales%d_%d" % (m, g0), align_bytes=64)
+            nc.vector.quantize_mx(out=e_codes[m, g0][:].bitcast(E5), scales=e_scales[m, g0][:], in_=e_grp[m, g0][:])
+
+        def v_interleave(i, part):
+            if part == 0:
+                v_grp[i] = work.tile([P, N, 4], BF16, name="v_grp" + V_ENG[i], bufs=V_BUFS[V_ENG[i]], align_bytes=64)
+            cols = slice(part * N // 2, (part + 1) * N // 2)
+            dst = v_grp[i][:, cols, :].rearrange("p (a b) t -> p a t b", b=4)
+            src = v_raw[i][:, :, cols].rearrange("p t (a b) -> p a t b", b=4)
+            if V_ENG[i] == "G":
+                dst = v_grp[i][:, cols, :]
+                src = v_raw[i][:, :, cols].rearrange("p t n -> p n t")
+            if V_ENG[i] == "V":
+                nc.vector.tensor_copy(out=dst, in_=src)
+            elif V_ENG[i] == "S":
+                nc.scalar.copy(out=dst, in_=src)
+            else:
+                nc.gpsimd.tensor_scalar(out=dst, in0=src, scalar1=1.0, scalar2=0.0, op0=ALU.mult, op1=ALU.add)
+
+        def v_quant(i):
+            v_codes[i] = keep.tile([P, N], U32, name="v_codes%d" % i, align_bytes=64)
+            v_scales[i] = keep.tile([P, N], U8, name="v_scales%d" % i, align_bytes=64)
+            nc.vector.quantize_mx(
+                out=v_codes[i][:].bitcast(E4), scales=v_scales[i][:], in_=v_grp[i][:].rearrange("p n t -> p (n t)")
+            )
+
+        def second_pass(m, h, g, tag="xo_bank"):
+            if g == 0:
+                o_bank[m, h] = psum.tile([P, N], F32, name=tag, bufs=3 if tag == "e_bank" else 2)
+            g0 = piece_of(m, g)[0]
+            cols = slice((g - g0) * P, (g - g0 + 1) * P)
+            nc.tensor.matmul_mx(
+                out=o_bank[m, h][:],
+                lhsT=e_codes[m, g0][:, cols].bitcast(E5),
+                lhsT_scale=e_scales[m, g0][:, cols],
+                rhs=v_codes[h * FG + g][:].bitcast(E4),
+                rhs_scale=v_scales[h * FG + g][:],
+                start=(g == 0),
+                stop=(g == FG - 1),
+            )
+
+        def second_product(m, h, tag="xo_bank"):
+            for g in range(FG):
+                second_pass(m, h, g, tag)
+
+        def finish(m, h, on_vector=False):
+            res = work.tile([P, N], F32, name="res", bufs=4, align_bytes=64)
+            if on_vector:
+                nc.vector.tensor_copy(out=res[:], in_=o_bank[m, h][:])
+            else:
+                nc.scalar.copy(out=res[:], in_=o_bank[m, h][:])
+            nc.sync.dma_start(out=out[m * P : (m + 1) * P, h * N : (h + 1) * N], in_=res[:])
+
+        def product_out(m, h, tag):
+            second_product(m, h, tag)
+            finish(m, h)
+
+        todo = [(m, h) for m in range(TILES - 1) for h in range(HALVES)]
+        v_done = 0
+        e_done = 0
+        last = TILES - 1
+        x_transpose(0)
+        x_copy(0)
+        x_transpose(1)
+        x_quant(0)
+        x_copy(1)
+        if "M" in MODES:
+            c_spread()
+        x_quant(1)
+        for s in range(TILES + 1):
+            live = s < TILES
+            turned = s >= 1 and MODES[s - 1] == "T"
+            mixed = live and MODES[s] == "M"
+            mixed_before = s >= 1 and MODES[s - 1] == "M"
+            xs = [m for m in range(2, TILES) if X_STEP[m] == s]
+            vs = [i for i in range(HALVES * FG) if V_STEP[i] == s]
+            vq = [i for i in range(HALVES * FG) if VQ_STEP[i] == s]
+            ready = [(m, h) for m, h in todo if m < e_done and all(h * FG + g in v_codes for g in range(FG))]
+            ready = ready[: S2_COUNT[s]]
+            for mh in ready:
+                todo.remove(mh)
+
+            s_jobs = []
+            if live:
+                first_product(s)
+            if mixed_before:
+                th_transpose(s - 1, FG - 1)
+                e_transpose(s - 1)
+                s_jobs.append((e_copy, (s - 1, 0, 2)))
+            if turned:
+                for g in range(FG):
+                    th_transpose(s - 1, g)
+            for m in xs:
+                x_transpose(m)
+                s_jobs.append((x_copy, (m,)))
+            for j, mh in enumerate(ready):
+                s_jobs.append((product_out, (mh[0], mh[1], "e_bank" if j == 2 and not turned else "xo_bank")))
+            for i in vs:
+                if V_ENG[i] == "S":
+                    s_jobs.extend([(v_interleave, (i, 0)), (v_interleave, (i, 1))])
+            cuts = [min(sum(SHARE[s][: g + 1]), len(s_jobs)) for g in range(FG)] + [len(s_jobs)]
+            for job, args in s_jobs[: cuts[0]]:
+                job(*args)
+            for i in vs:
+                if V_ENG[i] == "G":
+                    v_interleave(i, 0)
+                    v_interleave(i, 1)
+            for g in range(FG):
+                if live:
+                    subtract(s, g)
+                    tanh(s, g)
+                for job, args in s_jobs[cuts[g] : cuts[g + 1]]:
+                    job(*args)
+                if turned:
+                    weigh_turned(s - 1, g)
+                if mixed_before and g == 0:
+                    weigh_turned(s - 1, FG - 1)
+                if mixed and g == 1:
+                    weigh(s, 0)
+                if not live and g > 0:
+                    e_quant(last, g - 1, g)
+            for i in vs:
+                if V_ENG[i] == "V":
+                    v_interleave(i, 0)
+                    v_interleave(i, 1)
+            for m in range(2, TILES):
+                if XQ_STEP[m] == s:
+                    x_quant(m)
+            if 0 < s < TILES:
+                e_quant(s - 1, 0, 2)
+                e_quant(s - 1, 2, 3)
+                e_done = s
+            for i in vq:
+                v_quant(i)
+            if mixed:
+                weigh(s, 1)
+        e_quant(last, FG - 1, FG)
+        for j, mh in enumerate(todo):
+            second_product(*mh)
+            finish(*mh)
+        for g in range(FG):
+            for h in range(HALVES):
+                second_pass(last, h, g, "e_bank")
+        finish(last, 0)
+        finish(last, 1, on_vector=True)

@@ -11,29 +11,37 @@ BF16 = mybir.dt.bfloat16
 I32 = mybir.dt.int32
 U32 = mybir.dt.uint32
 U8 = mybir.dt.uint8
-E4 = mybir.dt.float8_e4m3fn_x4
-E5 = mybir.dt.float8_e5m2_x4
-E2 = mybir.dt.float4_e2m1fn_x4
+E4M3 = mybir.dt.float8_e4m3fn_x4
+E5M2 = mybir.dt.float8_e5m2_x4
+E2M1 = mybir.dt.float4_e2m1fn_x4
 ALU = mybir.AluOpType
 ACT = mybir.ActivationFunctionType
 
 P = 128
 N = 512
+SLOTS = 4
 TILES = M // P
-XG = D // N
-FG = F // N
+LAST = TILES - 1
+X_PASSES = D // N
+GROUPS = F // N
 HALVES = D // N
+CHUNKS = HALVES * GROUPS
 
-MODES = "TTTTMMMT"
-X_STEP = [0, 0, 0, 1, 1, 2, 2, 3]
-XQ_STEP = [0, 0, 0, 1, 2, 3, 4, 5]
-V_ENG = "VGSGSG"
-V_STEP = [0, 1, 1, 2, 2, 3]
-VQ_STEP = [1, 1, 2, 2, 3, 3]
-V_BUFS = {"V": 3, "S": 4, "G": 1}
-S2_COUNT = [0, 0, 0, 2, 3, 3, 2, 2, 2]
-SHARE = [[0, 0, 0], [0, 0, 1], [0, 0, 1], [1, 1, 1], [0, 1, 1], [0, 2, 1], [0, 1, 1], [0, 1, 0], [0, 2, 1]]
-LOAD_ORDER = "x0 x1 c w0 s y0a w1 y0b x2 v0 y1 v1 x3 x4 v2 y2 v3 x5 x6 x7 v4 y3 v5 y4 y5 y6 y7"
+EARLY_STEPS = 3
+ROWS_GROUPS = 2
+PRODUCTS_PER_STEP = 3
+
+
+def rows_groups(m):
+    return ROWS_GROUPS if EARLY_STEPS < m < LAST else 0
+
+
+def quantise_pieces(m):
+    return [(g, g + 1) for g in range(GROUPS)] if m == LAST else [(0, 2), (2, 3)]
+
+
+def x_tiles_of_step(s):
+    return [m for m in range(2, TILES) if (m - 1) // 2 == s]
 
 
 def tile_data2vec_head_backward_s9_kernel(tc, x, w_words, w_scales, y, c, v, out):
@@ -45,308 +53,299 @@ def tile_data2vec_head_backward_s9_kernel(tc, x, w_words, w_scales, y, c, v, out
         ctx.enter_context(tc.manual_schedule())
 
         x_raw = [keep.tile([P, D], BF16, name="x_raw%d" % m, align_bytes=64) for m in range(TILES)]
-        y_raw = [keep.tile([P, F], BF16, name="y_raw%d" % m, align_bytes=64) for m in range(1, TILES)]
+        y_raw = {m: keep.tile([P, F], BF16, name="y_raw%d" % m, align_bytes=64) for m in range(1, TILES)}
         y_first = keep.tile([P, N], BF16, name="y_first", align_bytes=64)
         y_rest = keep.tile([P, F - N], BF16, name="y_rest", align_bytes=64)
-        w_first = keep.tile([P, XG, 2 * N], U8, name="w_first", align_bytes=64)
-        w_rest = keep.tile([P, XG, 2 * (F - N)], U8, name="w_rest", align_bytes=64)
-        w_plane = keep.tile([P, XG, F], U8, name="w_plane", align_bytes=64)
-        v_raw = [keep.tile([P, 4, N], BF16, name="v_raw%d" % i, align_bytes=64) for i in range(HALVES * FG)]
-        c_col = keep.tile([P, FG, 16], BF16, name="c_col", align_bytes=64)
-        c_row = keep.tile([P, 2 * N], BF16, name="c_row", align_bytes=64)
+        w_first = keep.tile([P, X_PASSES, 2 * N], U8, name="w_first", align_bytes=64)
+        w_rest = keep.tile([P, X_PASSES, 2 * (F - N)], U8, name="w_rest", align_bytes=64)
+        w_scale = keep.tile([P, X_PASSES, F], U8, name="w_scale", align_bytes=64)
+        v_raw = [keep.tile([P, SLOTS, N], BF16, name="v_raw%d" % i, align_bytes=64) for i in range(CHUNKS)]
+        c_col = keep.tile([P, GROUPS, 16], BF16, name="c_col", align_bytes=64)
+        c_row = keep.tile([P, ROWS_GROUPS * N], BF16, name="c_row", align_bytes=64)
         ident = keep.tile([P, P], F32, name="ident", align_bytes=64)
         warm = keep.tile([P, 16], F32, name="warm", align_bytes=64)
 
         def y_cols(m, g):
             if m > 0:
-                return y_raw[m - 1][:, g * N : (g + 1) * N]
+                return y_raw[m][:, g * N : (g + 1) * N]
             return y_first[:] if g == 0 else y_rest[:, (g - 1) * N : g * N]
 
-        def w_cols(kg, g):
+        def w_cols(kp, g):
             if g == 0:
-                return w_first[:, kg, :]
-            return w_rest[:, kg, (g - 1) * 2 * N : g * 2 * N]
+                return w_first[:, kp, :]
+            return w_rest[:, kp, (g - 1) * 2 * N : g * 2 * N]
 
-        nc.vector.memset(w_plane[:].rearrange("p g n -> p (g n)").bitcast(I32), 0)
+        def load_x(m):
+            nc.sync.dma_start(out=x_raw[m][:], in_=x[m * P : (m + 1) * P, :])
+
+        def load_y(m):
+            nc.sync.dma_start(out=y_raw[m][:], in_=y[m * P : (m + 1) * P, :])
+
+        def load_v(i):
+            h, g = divmod(i, GROUPS)
+            rows = v[g * N : (g + 1) * N, h * N : (h + 1) * N]
+            nc.sync.dma_start(out=v_raw[i][:], in_=rows.rearrange("(p t) n -> p t n", t=SLOTS))
+
+        nc.vector.memset(w_scale[:].rearrange("p g n -> p (g n)").bitcast(I32), 0)
         nc.vector.memset(warm[:, 0:1], 0.0)
         make_identity(nc, ident[:])
-        nc.scalar.activation(out=warm[:, 8:9], in_=warm[:, 0:1], func=ACT.Tanh)
 
         w_i32 = w_words.bitcast(I32).rearrange("g p n -> p g n")
         s_i32 = w_scales.bitcast(I32).rearrange("g q n -> q g n")
-        for item in LOAD_ORDER.split(" "):
-            if item == "w0":
-                nc.sync.dma_start(out=w_first[:].bitcast(I32), in_=w_i32[:, :, 0 : N // 2])
-            elif item == "w1":
-                nc.sync.dma_start(out=w_rest[:].bitcast(I32), in_=w_i32[:, :, N // 2 : F // 2])
-            elif item == "s":
-                for q in range(4):
-                    nc.sync.dma_start(out=w_plane[32 * q : 32 * q + 4].bitcast(I32), in_=s_i32[4 * q : 4 * q + 4])
-            elif item == "y0a":
-                nc.sync.dma_start(out=y_first[:], in_=y[0:P, 0:N])
-            elif item == "y0b":
-                nc.sync.dma_start(out=y_rest[:], in_=y[0:P, N:F])
-            elif item == "c":
-                nc.sync.dma_start(out=c_col[:, :, 0:4], in_=c.rearrange("(g p t) -> p g t", p=P, t=4))
-            elif item.startswith("x"):
-                m = int(item[1:])
-                nc.sync.dma_start(out=x_raw[m][:], in_=x[m * P : (m + 1) * P, :])
-            elif item.startswith("y"):
-                m = int(item[1:])
-                nc.sync.dma_start(out=y_raw[m - 1][:], in_=y[m * P : (m + 1) * P, :])
-            else:
-                i = int(item[1:])
-                h, g = divmod(i, FG)
-                nc.sync.dma_start(
-                    out=v_raw[i][:],
-                    in_=v[g * N : (g + 1) * N, h * N : (h + 1) * N].rearrange("(p t) n -> p t n", t=4),
-                )
+        load_x(0)
+        for quad in range(4):
+            nc.sync.dma_start(
+                out=w_scale[32 * quad : 32 * quad + 4].bitcast(I32), in_=s_i32[4 * quad : 4 * quad + 4]
+            )
+        nc.sync.dma_start(out=w_first[:].bitcast(I32), in_=w_i32[:, :, 0 : N // 2])
+        nc.sync.dma_start(out=y_first[:], in_=y[0:P, 0:N])
+        load_x(1)
+        nc.sync.dma_start(out=w_rest[:].bitcast(I32), in_=w_i32[:, :, N // 2 : F // 2])
+        nc.sync.dma_start(out=y_rest[:], in_=y[0:P, N:F])
+        nc.sync.dma_start(out=c_col[:, :, 0:SLOTS], in_=c.rearrange("(g p t) -> p g t", p=P, t=SLOTS))
+        for s in range(EARLY_STEPS):
+            for m in x_tiles_of_step(s):
+                load_x(m)
+            load_v(2 * s)
+            load_y(s + 1)
+            load_v(2 * s + 1)
+        load_x(LAST)
+        for m in range(EARLY_STEPS + 1, TILES):
+            load_y(m)
 
-        x_bank, x_grp, x_codes, x_scales = {}, {}, {}, {}
-        pred, diff, th, e_rows, e_bank, e_grp, e_codes, e_scales = {}, {}, {}, {}, {}, {}, {}, {}
-        v_grp, v_codes, v_scales, o_bank = {}, {}, {}, {}
+        nc.scalar.activation(out=warm[:, 8:9], in_=warm[:, 0:1], func=ACT.Tanh)
+
+        x_bank, x_inter, x_codes, x_scale = {}, {}, {}, {}
+        pred, diff, th, e_rows, e_bank, e_inter, e_codes, e_scale = {}, {}, {}, {}, {}, {}, {}, {}
+        v_inter, v_codes, v_scale, o_bank = {}, {}, {}, {}
 
         def x_transpose(m):
-            x_bank[m] = psum.tile([P, XG, 2, P], F32, name="xo_bank", bufs=2)
+            x_bank[m] = psum.tile([P, X_PASSES, 2, P], F32, name="xo_bank", bufs=2)
             words = x_raw[m][:].bitcast(F32)
-            for g in range(XG):
+            for kp in range(X_PASSES):
                 for u in range(2):
-                    nc.tensor.transpose(x_bank[m][:, g, u, :], words[:, 256 * g + u : 256 * (g + 1) : 2], ident[:])
+                    in_words = words[:, kp * N // 2 + u : (kp + 1) * N // 2 : 2]
+                    nc.tensor.transpose(x_bank[m][:, kp, u, :], in_words, ident[:])
 
         def x_copy(m):
-            x_grp[m] = work.tile([P, D], BF16, name="x_grp", bufs=TILES, align_bytes=64)
+            x_inter[m] = work.tile([P, D], BF16, name="x_inter", bufs=TILES, align_bytes=64)
             nc.scalar.copy(
-                out=x_grp[m][:].bitcast(F32).rearrange("p (g r u) -> p g r u", g=XG, u=2),
+                out=x_inter[m][:].bitcast(F32).rearrange("p (g r u) -> p g r u", g=X_PASSES, u=2),
                 in_=x_bank[m][:].rearrange("p g u r -> p g r u"),
             )
 
-        def x_quant(m):
-            x_codes[m] = work.tile([P, D // 4], U32, name="x_codes", bufs=3, align_bytes=64)
-            x_scales[m] = work.tile([P, D // 4], U8, name="x_scales", bufs=3, align_bytes=64)
-            nc.vector.quantize_mx(out=x_codes[m][:].bitcast(E4), scales=x_scales[m][:], in_=x_grp[m][:])
+        def x_quantise(m):
+            x_codes[m] = work.tile([P, D // SLOTS], U32, name="x_codes", bufs=3, align_bytes=64)
+            x_scale[m] = work.tile([P, D // SLOTS], U8, name="x_scale", bufs=3, align_bytes=64)
+            nc.vector.quantize_mx(out=x_codes[m][:].bitcast(E4M3), scales=x_scale[m][:], in_=x_inter[m][:])
 
         def c_spread():
             words = c_col[:].bitcast(F32)
-            bank = psum.tile([P, 4, P], F32, name="e_bank", bufs=3)
-            for g in range(2):
+            bank = psum.tile([P, ROWS_GROUPS, 2, P], F32, name="xo_bank", bufs=2)
+            for g in range(ROWS_GROUPS):
                 for u in range(2):
-                    nc.tensor.transpose(bank[:, 2 * g + u, :], words[:, g, u : u + 1].to_broadcast([P, P]), ident[:])
-            nc.scalar.copy(out=c_row[:].bitcast(F32), in_=bank[:].rearrange("p a r -> p (a r)"))
+                    nc.tensor.transpose(bank[:, g, u, :], words[:, g, u : u + 1].to_broadcast([P, P]), ident[:])
+            nc.scalar.copy(out=c_row[:].bitcast(F32), in_=bank[:].rearrange("p g u r -> p (g u r)"))
 
-        def first_product(m):
-            for g in range(FG):
-                pred[m, g] = psum.tile([P, N], F32, name="pred", bufs=3)
-                for kg in range(XG):
-                    nc.tensor.matmul_mx(
-                        out=pred[m, g][:],
-                        lhsT=x_codes[m][:, kg * P : (kg + 1) * P].bitcast(E4),
-                        lhsT_scale=x_scales[m][:, kg * P : (kg + 1) * P],
-                        rhs=w_cols(kg, g).bitcast(E2),
-                        rhs_scale=w_plane[:, kg, g * N : (g + 1) * N],
-                        start=(kg == 0),
-                        stop=(kg == XG - 1),
-                    )
+        def first_product(m, g):
+            pred[m, g] = psum.tile([P, N], F32, name="pred", bufs=3)
+            for kp in range(X_PASSES):
+                nc.tensor.matmul_mx(
+                    out=pred[m, g][:],
+                    lhsT=x_codes[m][:, kp * P : (kp + 1) * P].bitcast(E4M3),
+                    lhsT_scale=x_scale[m][:, kp * P : (kp + 1) * P],
+                    rhs=w_cols(kp, g).bitcast(E2M1),
+                    rhs_scale=w_scale[:, kp, g * N : (g + 1) * N],
+                    start=(kp == 0),
+                    stop=(kp == X_PASSES - 1),
+                )
 
         def subtract(m, g):
             diff[m, g] = work.tile([P, N], F32, name="diff", bufs=3, align_bytes=64)
-            u, e = (4, 1) if MODES[m] == "T" or g == FG - 1 else (2, 2)
             nc.vector.tensor_tensor(
-                out=diff[m, g][:].rearrange("p (u q e) -> p u q e", u=u, e=e),
-                in0=pred[m, g][:].rearrange("p (q u e) -> p u q e", u=u, e=e),
-                in1=y_cols(m, g).rearrange("p (q u e) -> p u q e", u=u, e=e),
+                out=diff[m, g][:].rearrange("p (u q e) -> p u q e", u=2, e=2),
+                in0=pred[m, g][:].rearrange("p (q u e) -> p u q e", u=2, e=2),
+                in1=y_cols(m, g).rearrange("p (q u e) -> p u q e", u=2, e=2),
                 op=ALU.subtract,
             )
 
         def tanh(m, g):
-            th[m, g] = work.tile([P, N], F32, name="th", bufs=4, align_bytes=64)
-            nc.scalar.activation(out=th[m, g][:], in_=diff[m, g][:], func=ACT.Tanh)
-
-        def weigh(m, g):
-            e_rows[m, g] = work.tile([P, N], BF16, name="e_rows", bufs=6, align_bytes=64)
-            nc.vector.tensor_tensor(
-                out=e_rows[m, g][:], in0=th[m, g][:], in1=c_row[:, g * N : (g + 1) * N], op=ALU.mult
-            )
-
-        def e_transpose(m):
-            e_bank[m, 0] = psum.tile([P, 2, 2, P], F32, name="e_bank", bufs=3)
-            for g in range(2):
-                words = e_rows[m, g][:].bitcast(F32)
-                for u in range(2):
-                    nc.tensor.transpose(e_bank[m, 0][:, g, u, :], words[:, u * P : (u + 1) * P], ident[:])
+            if g == 0:
+                th[m] = work.tile([P, F], F32, name="th", bufs=2, align_bytes=64)
+            dst, src = th[m][:, g * N : (g + 1) * N], diff[m, g][:]
+            if m >= EARLY_STEPS and g >= rows_groups(m):
+                dst = dst.rearrange("p (u e q) -> p u e q", u=2, e=2)
+                src = src.rearrange("p (u q e) -> p u e q", u=2, e=2)
+            nc.scalar.activation(out=dst, in_=src, func=ACT.Tanh)
 
         def th_transpose(m, g):
-            e_bank[m, g] = psum.tile([P, 4, P], F32, name="pred" if m == TILES - 1 else "e_bank", bufs=3)
-            for t in range(4):
-                nc.tensor.transpose(e_bank[m, g][:, t, :], th[m, g][:, t * P : (t + 1) * P], ident[:])
-
-        def pieces(m):
-            return ((0, 1), (1, 2), (2, 3)) if m == TILES - 1 else ((0, 2), (2, 3))
+            e_bank[m, g] = psum.tile([P, SLOTS, P], F32, name="pred" if m == LAST else "e_bank", bufs=3)
+            cols = th[m][:, g * N : (g + 1) * N]
+            for t in range(SLOTS):
+                u, e = divmod(t, 2)
+                slot = cols[:, t * P : (t + 1) * P] if m >= EARLY_STEPS else cols[:, u * 2 * P + e : (u + 1) * 2 * P : 2]
+                nc.tensor.transpose(e_bank[m, g][:, t, :], slot, ident[:])
 
         def piece_of(m, g):
-            return [(g0, g1) for g0, g1 in pieces(m) if g0 <= g < g1][0]
+            return [(g0, g1) for g0, g1 in quantise_pieces(m) if g0 <= g < g1][0]
 
         def weigh_turned(m, g):
             g0, g1 = piece_of(m, g)
             if g == g0:
-                e_grp[m, g0] = work.tile([P, (g1 - g0) * N], BF16, name="e_grp%d" % g0, bufs=2, align_bytes=64)
+                e_inter[m, g0] = work.tile([P, (g1 - g0) * N], BF16, name="e_inter%d" % g0, bufs=2, align_bytes=64)
             nc.vector.tensor_tensor(
-                out=e_grp[m, g0][:, (g - g0) * N : (g - g0 + 1) * N].rearrange("p (r t) -> p r t", t=4),
-                in0=e_bank[m, g][:].rearrange("p t r -> p r t"),
-                in1=c_col[:, g : g + 1, 0:4].to_broadcast([P, P, 4]),
+                out=e_inter[m, g0][:, (g - g0) * N : (g - g0 + 1) * N].rearrange("p (a b t) -> p a t b", b=2, t=SLOTS),
+                in0=e_bank[m, g][:].rearrange("p t (a b) -> p a t b", b=2),
+                in1=c_col[:, g : g + 1, 0:SLOTS].unsqueeze(3).to_broadcast([P, P // 2, SLOTS, 2]),
                 op=ALU.mult,
             )
 
-        def e_copy(m, g0, g1):
-            e_grp[m, g0] = work.tile([P, (g1 - g0) * N], BF16, name="e_grp%d" % g0, bufs=2, align_bytes=64)
+        def weigh_rows(m):
+            e_rows[m] = work.tile([P, ROWS_GROUPS * N], BF16, name="e_rows", bufs=2, align_bytes=64)
+            nc.vector.tensor_tensor(out=e_rows[m][:], in0=th[m][:, 0 : ROWS_GROUPS * N], in1=c_row[:], op=ALU.mult)
+
+        def rows_transpose(m):
+            e_bank[m, 0] = psum.tile([P, ROWS_GROUPS, 2, P], F32, name="e_bank", bufs=3)
+            words = e_rows[m][:].bitcast(F32).rearrange("p (g u q) -> p g u q", g=ROWS_GROUPS, u=2)
+            for g in range(ROWS_GROUPS):
+                for u in range(2):
+                    nc.tensor.transpose(e_bank[m, 0][:, g, u, :], words[:, g, u, :], ident[:])
+
+        def rows_copy(m):
+            e_inter[m, 0] = work.tile([P, ROWS_GROUPS * N], BF16, name="e_inter0", bufs=2, align_bytes=64)
             nc.scalar.copy(
-                out=e_grp[m, g0][:].bitcast(F32).rearrange("p (g r u) -> p g r u", r=P, u=2),
-                in_=e_bank[m, g0][:, 0 : g1 - g0].rearrange("p g u r -> p g r u"),
+                out=e_inter[m, 0][:].bitcast(F32).rearrange("p (g r u) -> p g r u", r=P, u=2),
+                in_=e_bank[m, 0][:].rearrange("p g u r -> p g r u"),
             )
 
-        def e_quant(m, g0, g1):
+        def e_quantise(m, g0, g1):
             e_codes[m, g0] = keep.tile([P, (g1 - g0) * P], U32, name="e_codes%d_%d" % (m, g0), align_bytes=64)
-            e_scales[m, g0] = keep.tile([P, (g1 - g0) * P], U8, name="e_scales%d_%d" % (m, g0), align_bytes=64)
-            nc.vector.quantize_mx(out=e_codes[m, g0][:].bitcast(E5), scales=e_scales[m, g0][:], in_=e_grp[m, g0][:])
+            e_scale[m, g0] = keep.tile([P, (g1 - g0) * P], U8, name="e_scale%d_%d" % (m, g0), align_bytes=64)
+            nc.vector.quantize_mx(out=e_codes[m, g0][:].bitcast(E5M2), scales=e_scale[m, g0][:], in_=e_inter[m, g0][:])
 
         def v_interleave(i, part):
-            if part == 0:
-                v_grp[i] = work.tile([P, N, 4], BF16, name="v_grp" + V_ENG[i], bufs=V_BUFS[V_ENG[i]], align_bytes=64)
             cols = slice(part * N // 2, (part + 1) * N // 2)
-            dst = v_grp[i][:, cols, :].rearrange("p (a b) t -> p a t b", b=4)
-            src = v_raw[i][:, :, cols].rearrange("p t (a b) -> p a t b", b=4)
-            if V_ENG[i] == "G":
-                dst = v_grp[i][:, cols, :]
+            if i % 2 == 1:
+                if part == 0:
+                    v_inter[i] = work.tile([P, N, SLOTS], BF16, name="v_inter_gpsimd", bufs=1, align_bytes=64)
                 src = v_raw[i][:, :, cols].rearrange("p t n -> p n t")
-            if V_ENG[i] == "V":
+                nc.gpsimd.tensor_scalar(
+                    out=v_inter[i][:, cols, :], in0=src, scalar1=1.0, scalar2=0.0, op0=ALU.mult, op1=ALU.add
+                )
+                return
+            if part == 0:
+                v_inter[i] = work.tile([P, N, SLOTS], BF16, name="v_inter", bufs=3, align_bytes=64)
+            dst = v_inter[i][:, cols, :].rearrange("p (a b) t -> p a t b", b=4)
+            src = v_raw[i][:, :, cols].rearrange("p t (a b) -> p a t b", b=4)
+            if i == 0:
                 nc.vector.tensor_copy(out=dst, in_=src)
-            elif V_ENG[i] == "S":
+            else:
                 nc.scalar.copy(out=dst, in_=src)
-            else:
-                nc.gpsimd.tensor_scalar(out=dst, in0=src, scalar1=1.0, scalar2=0.0, op0=ALU.mult, op1=ALU.add)
 
-        def v_quant(i):
+        def v_quantise(i):
             v_codes[i] = keep.tile([P, N], U32, name="v_codes%d" % i, align_bytes=64)
-            v_scales[i] = keep.tile([P, N], U8, name="v_scales%d" % i, align_bytes=64)
+            v_scale[i] = keep.tile([P, N], U8, name="v_scale%d" % i, align_bytes=64)
             nc.vector.quantize_mx(
-                out=v_codes[i][:].bitcast(E4), scales=v_scales[i][:], in_=v_grp[i][:].rearrange("p n t -> p (n t)")
+                out=v_codes[i][:].bitcast(E4M3), scales=v_scale[i][:], in_=v_inter[i][:].rearrange("p n t -> p (n t)")
             )
 
-        def second_pass(m, h, g, tag="xo_bank"):
-            if g == 0:
-                o_bank[m, h] = psum.tile([P, N], F32, name=tag, bufs=3 if tag == "e_bank" else 2)
-            g0 = piece_of(m, g)[0]
-            cols = slice((g - g0) * P, (g - g0 + 1) * P)
-            nc.tensor.matmul_mx(
-                out=o_bank[m, h][:],
-                lhsT=e_codes[m, g0][:, cols].bitcast(E5),
-                lhsT_scale=e_scales[m, g0][:, cols],
-                rhs=v_codes[h * FG + g][:].bitcast(E4),
-                rhs_scale=v_scales[h * FG + g][:],
-                start=(g == 0),
-                stop=(g == FG - 1),
-            )
-
-        def second_product(m, h, tag="xo_bank"):
-            for g in range(FG):
-                second_pass(m, h, g, tag)
-
-        def finish(m, h, on_vector=False):
-            res = work.tile([P, N], F32, name="res", bufs=4, align_bytes=64)
-            if on_vector:
-                nc.vector.tensor_copy(out=res[:], in_=o_bank[m, h][:])
-            else:
-                nc.scalar.copy(out=res[:], in_=o_bank[m, h][:])
-            nc.sync.dma_start(out=out[m * P : (m + 1) * P, h * N : (h + 1) * N], in_=res[:])
+        def second_product(m, h, tag):
+            o_bank[m, h] = psum.tile([P, N], F32, name=tag, bufs=3 if tag == "e_bank" else 2)
+            for g in range(GROUPS):
+                g0 = piece_of(m, g)[0]
+                cols = slice((g - g0) * P, (g - g0 + 1) * P)
+                nc.tensor.matmul_mx(
+                    out=o_bank[m, h][:],
+                    lhsT=e_codes[m, g0][:, cols].bitcast(E5M2),
+                    lhsT_scale=e_scale[m, g0][:, cols],
+                    rhs=v_codes[h * GROUPS + g][:].bitcast(E4M3),
+                    rhs_scale=v_scale[h * GROUPS + g][:],
+                    start=(g == 0),
+                    stop=(g == GROUPS - 1),
+                )
 
         def product_out(m, h, tag):
             second_product(m, h, tag)
-            finish(m, h)
+            res = work.tile([P, N], F32, name="res", bufs=4, align_bytes=64)
+            nc.scalar.copy(out=res[:], in_=o_bank[m, h][:])
+            nc.sync.dma_start(out=out[m * P : (m + 1) * P, h * N : (h + 1) * N], in_=res[:])
 
-        todo = [(m, h) for m in range(TILES - 1) for h in range(HALVES)]
-        v_done = 0
-        e_done = 0
-        last = TILES - 1
         x_transpose(0)
         x_copy(0)
+        x_quantise(0)
+        first_product(0, 0)
         x_transpose(1)
-        x_quant(0)
         x_copy(1)
-        if "M" in MODES:
-            c_spread()
-        x_quant(1)
-        for s in range(TILES + 1):
-            live = s < TILES
-            turned = s >= 1 and MODES[s - 1] == "T"
-            mixed = live and MODES[s] == "M"
-            mixed_before = s >= 1 and MODES[s - 1] == "M"
-            xs = [m for m in range(2, TILES) if X_STEP[m] == s]
-            vs = [i for i in range(HALVES * FG) if V_STEP[i] == s]
-            vq = [i for i in range(HALVES * FG) if VQ_STEP[i] == s]
-            ready = [(m, h) for m, h in todo if m < e_done and all(h * FG + g in v_codes for g in range(FG))]
-            ready = ready[: S2_COUNT[s]]
-            for mh in ready:
-                todo.remove(mh)
+        for g in range(1, GROUPS):
+            first_product(0, g)
 
-            s_jobs = []
-            if live:
-                first_product(s)
-            if mixed_before:
-                th_transpose(s - 1, FG - 1)
-                e_transpose(s - 1)
-                s_jobs.append((e_copy, (s - 1, 0, 2)))
-            if turned:
-                for g in range(FG):
-                    th_transpose(s - 1, g)
-            for m in xs:
+        waiting = [(m, h) for m in range(LAST) for h in range(HALVES)]
+        for s in range(TILES + 1):
+            prev = s - 1
+            turned = range(rows_groups(prev), GROUPS) if s > 0 else range(0)
+            ready = [
+                (m, h) for m, h in waiting if (m, 0) in e_codes and (h + 1) * GROUPS - 1 in v_codes
+            ][:PRODUCTS_PER_STEP]
+            for product in ready:
+                waiting.remove(product)
+
+            if EARLY_STEPS < s < TILES:
+                for g in range(GROUPS):
+                    first_product(s, g)
+            for g in turned:
+                if s <= EARLY_STEPS:
+                    first_product(s, g)
+                th_transpose(prev, g)
+            jobs = []
+            if rows_groups(prev):
+                rows_transpose(prev)
+                jobs.append((rows_copy, prev))
+            for m in x_tiles_of_step(s):
                 x_transpose(m)
-                s_jobs.append((x_copy, (m,)))
-            for j, mh in enumerate(ready):
-                s_jobs.append((product_out, (mh[0], mh[1], "e_bank" if j == 2 and not turned else "xo_bank")))
-            for i in vs:
-                if V_ENG[i] == "S":
-                    s_jobs.extend([(v_interleave, (i, 0)), (v_interleave, (i, 1))])
-            cuts = [min(sum(SHARE[s][: g + 1]), len(s_jobs)) for g in range(FG)] + [len(s_jobs)]
-            for job, args in s_jobs[: cuts[0]]:
-                job(*args)
-            for i in vs:
-                if V_ENG[i] == "G":
-                    v_interleave(i, 0)
-                    v_interleave(i, 1)
-            for g in range(FG):
-                if live:
+                jobs.append((x_copy, m))
+            if s == 0:
+                jobs.append((c_spread,))
+            for j, (m, h) in enumerate(ready):
+                jobs.append((product_out, m, h, "e_bank" if j == 2 and rows_groups(prev) else "xo_bank"))
+            if 0 < s < EARLY_STEPS:
+                jobs.extend([(v_interleave, 2 * s, 0), (v_interleave, 2 * s, 1)])
+            if 0 < s <= EARLY_STEPS:
+                v_interleave(2 * s - 1, 0)
+                v_interleave(2 * s - 1, 1)
+
+            cuts = [0, 1, 1 if s == LAST else 2, len(jobs)]
+            for g in range(GROUPS):
+                if s < TILES:
                     subtract(s, g)
                     tanh(s, g)
-                for job, args in s_jobs[cuts[g] : cuts[g + 1]]:
-                    job(*args)
-                if turned:
-                    weigh_turned(s - 1, g)
-                if mixed_before and g == 0:
-                    weigh_turned(s - 1, FG - 1)
-                if mixed and g == 1:
-                    weigh(s, 0)
-                if not live and g > 0:
-                    e_quant(last, g - 1, g)
-            for i in vs:
-                if V_ENG[i] == "V":
-                    v_interleave(i, 0)
-                    v_interleave(i, 1)
-            for m in range(2, TILES):
-                if XQ_STEP[m] == s:
-                    x_quant(m)
+                for job in jobs[cuts[g] : cuts[g + 1]]:
+                    job[0](*job[1:])
+                if g < len(turned):
+                    weigh_turned(prev, turned[g])
+                if s == 0 and g == 0:
+                    x_quantise(1)
+                if s == TILES and g > 0:
+                    e_quantise(LAST, g - 1, g)
+
+            if s == 0:
+                v_interleave(0, 0)
+                v_interleave(0, 1)
+            if s + 2 < TILES:
+                x_quantise(s + 2)
             if 0 < s < TILES:
-                e_quant(s - 1, 0, 2)
-                e_quant(s - 1, 2, 3)
-                e_done = s
-            for i in vq:
-                v_quant(i)
-            if mixed:
-                weigh(s, 1)
-        e_quant(last, FG - 1, FG)
-        for j, mh in enumerate(todo):
-            second_product(*mh)
-            finish(*mh)
-        for g in range(FG):
-            for h in range(HALVES):
-                second_pass(last, h, g, "e_bank")
-        finish(last, 0)
-        finish(last, 1, on_vector=True)
+                for g0, g1 in quantise_pieces(prev):
+                    e_quantise(prev, g0, g1)
+            if 0 < s <= EARLY_STEPS:
+                v_quantise(2 * s - 2)
+                v_quantise(2 * s - 1)
+            if rows_groups(s):
+                weigh_rows(s)
+
+        e_quantise(LAST, GROUPS - 1, GROUPS)
+        product_out(LAST, 0, "e_bank")
+        second_product(LAST, 1, "e_bank")
+        for part in range(2):
+            cols = slice(part * N // 2, (part + 1) * N // 2)
+            res_last = work.tile([P, N // 2], F32, name="res_last", bufs=2, align_bytes=64)
+            nc.vector.tensor_copy(out=res_last[:], in_=o_bank[LAST, 1][:, cols])
+            nc.sync.dma_start(out=out[LAST * P :, N + cols.start : N + cols.stop], in_=res_last[:])

@@ -63,7 +63,6 @@ def tile_data2vec_head_backward_s9_kernel(tc, x, w_words, w_scales, y, c, v, out
         c_col = keep.tile([P, GROUPS, 16], BF16, name="c_col", align_bytes=64)
         c_row = keep.tile([P, ROWS_GROUPS * N], BF16, name="c_row", align_bytes=64)
         ident = keep.tile([P, P], F32, name="ident", align_bytes=64)
-        warm = keep.tile([P, 16], F32, name="warm", align_bytes=64)
 
         def y_cols(m, g):
             if m > 0:
@@ -87,7 +86,6 @@ def tile_data2vec_head_backward_s9_kernel(tc, x, w_words, w_scales, y, c, v, out
             nc.sync.dma_start(out=v_raw[i][:], in_=rows.rearrange("(p t) n -> p t n", t=SLOTS))
 
         nc.vector.memset(w_scale[:].rearrange("p g n -> p (g n)").bitcast(I32), 0)
-        nc.vector.memset(warm[:, 0:1], 0.0)
         make_identity(nc, ident[:])
 
         w_i32 = w_words.bitcast(I32).rearrange("g p n -> p g n")
@@ -112,8 +110,6 @@ def tile_data2vec_head_backward_s9_kernel(tc, x, w_words, w_scales, y, c, v, out
         load_x(LAST)
         for m in range(EARLY_STEPS + 1, TILES):
             load_y(m)
-
-        nc.scalar.activation(out=warm[:, 8:9], in_=warm[:, 0:1], func=ACT.Tanh)
 
         x_bank, x_inter, x_codes, x_scale = {}, {}, {}, {}
         pred, diff, th, e_rows, e_bank, e_inter, e_codes, e_scale = {}, {}, {}, {}, {}, {}, {}, {}

@@ -33,7 +33,7 @@ PRODUCTS_PER_STEP = 3
 
 
 def rows_groups(m):
-    return ROWS_GROUPS if EARLY_STEPS < m < LAST else 0
+    return ROWS_GROUPS if EARLY_STEPS <= m < LAST else 0
 
 
 def quantise_pieces(m):
@@ -41,7 +41,7 @@ def quantise_pieces(m):
 
 
 def x_tiles_of_step(s):
-    return [m for m in range(2, TILES) if (m - 1) // 2 == s]
+    return [m for m in range(2, TILES) if (2 * m - 3) // 3 == s]
 
 
 def tile_data2vec_head_backward_s9_kernel(tc, x, w_words, w_scales, y, c, v, out):
@@ -106,8 +106,10 @@ def tile_data2vec_head_backward_s9_kernel(tc, x, w_words, w_scales, y, c, v, out
                 load_x(m)
             load_v(2 * s)
             load_y(s + 1)
+            if s + 1 == EARLY_STEPS:
+                for m in x_tiles_of_step(EARLY_STEPS):
+                    load_x(m)
             load_v(2 * s + 1)
-        load_x(LAST)
         for m in range(EARLY_STEPS + 1, TILES):
             load_y(m)
 
@@ -157,30 +159,25 @@ def tile_data2vec_head_backward_s9_kernel(tc, x, w_words, w_scales, y, c, v, out
                 )
 
         def subtract(m, g):
+            runs, pair = (2, 2) if g < rows_groups(m) else (SLOTS, 1)
             diff[m, g] = work.tile([P, N], F32, name="diff", bufs=3, align_bytes=64)
             nc.vector.tensor_tensor(
-                out=diff[m, g][:].rearrange("p (u q e) -> p u q e", u=2, e=2),
-                in0=pred[m, g][:].rearrange("p (q u e) -> p u q e", u=2, e=2),
-                in1=y_cols(m, g).rearrange("p (q u e) -> p u q e", u=2, e=2),
+                out=diff[m, g][:].rearrange("p (u q e) -> p u q e", u=runs, e=pair),
+                in0=pred[m, g][:].rearrange("p (q u e) -> p u q e", u=runs, e=pair),
+                in1=y_cols(m, g).rearrange("p (q u e) -> p u q e", u=runs, e=pair),
                 op=ALU.subtract,
             )
 
         def tanh(m, g):
             if g == 0:
                 th[m] = work.tile([P, F], F32, name="th", bufs=2, align_bytes=64)
-            dst, src = th[m][:, g * N : (g + 1) * N], diff[m, g][:]
-            if m >= EARLY_STEPS and g >= rows_groups(m):
-                dst = dst.rearrange("p (u e q) -> p u e q", u=2, e=2)
-                src = src.rearrange("p (u q e) -> p u e q", u=2, e=2)
-            nc.scalar.activation(out=dst, in_=src, func=ACT.Tanh)
+            nc.scalar.activation(out=th[m][:, g * N : (g + 1) * N], in_=diff[m, g][:], func=ACT.Tanh)
 
         def th_transpose(m, g):
             e_bank[m, g] = psum.tile([P, SLOTS, P], F32, name="pred" if m == LAST else "e_bank", bufs=3)
-            cols = th[m][:, g * N : (g + 1) * N]
             for t in range(SLOTS):
-                u, e = divmod(t, 2)
-                slot = cols[:, t * P : (t + 1) * P] if m >= EARLY_STEPS else cols[:, u * 2 * P + e : (u + 1) * 2 * P : 2]
-                nc.tensor.transpose(e_bank[m, g][:, t, :], slot, ident[:])
+                first = g * N + t * P
+                nc.tensor.transpose(e_bank[m, g][:, t, :], th[m][:, first : first + P], ident[:])
 
         def piece_of(m, g):
             return [(g0, g1) for g0, g1 in quantise_pieces(m) if g0 <= g < g1][0]
@@ -190,9 +187,9 @@ def tile_data2vec_head_backward_s9_kernel(tc, x, w_words, w_scales, y, c, v, out
             if g == g0:
                 e_inter[m, g0] = work.tile([P, (g1 - g0) * N], BF16, name="e_inter%d" % g0, bufs=2, align_bytes=64)
             nc.vector.tensor_tensor(
-                out=e_inter[m, g0][:, (g - g0) * N : (g - g0 + 1) * N].rearrange("p (a b t) -> p a t b", b=2, t=SLOTS),
-                in0=e_bank[m, g][:].rearrange("p t (a b) -> p a t b", b=2),
-                in1=c_col[:, g : g + 1, 0:SLOTS].unsqueeze(3).to_broadcast([P, P // 2, SLOTS, 2]),
+                out=e_inter[m, g0][:, (g - g0) * N : (g - g0 + 1) * N].rearrange("p (r t) -> p r t", t=SLOTS),
+                in0=e_bank[m, g][:].rearrange("p t r -> p r t"),
+                in1=c_col[:, g : g + 1, 0:SLOTS].to_broadcast([P, P, SLOTS]),
                 op=ALU.mult,
             )
 
@@ -292,23 +289,30 @@ def tile_data2vec_head_backward_s9_kernel(tc, x, w_words, w_scales, y, c, v, out
                 if s <= EARLY_STEPS:
                     first_product(s, g)
                 th_transpose(prev, g)
+                if s == EARLY_STEPS and g < len(x_tiles_of_step(s)):
+                    x_transpose(x_tiles_of_step(s)[g])
             jobs = []
             if rows_groups(prev):
                 rows_transpose(prev)
                 jobs.append((rows_copy, prev))
             for m in x_tiles_of_step(s):
-                x_transpose(m)
+                if s < EARLY_STEPS:
+                    x_transpose(m)
                 jobs.append((x_copy, m))
             if s == 0:
                 jobs.append((c_spread,))
             for j, (m, h) in enumerate(ready):
-                jobs.append((product_out, m, h, "e_bank" if j == 2 and rows_groups(prev) else "xo_bank"))
+                spare = s == TILES or (j == PRODUCTS_PER_STEP - 1 and rows_groups(prev) > 0)
+                jobs.append((product_out, m, h, "e_bank" if spare else "xo_bank"))
             if 0 < s < EARLY_STEPS:
                 jobs.extend([(v_interleave, 2 * s, 0), (v_interleave, 2 * s, 1)])
             if 0 < s <= EARLY_STEPS:
                 v_interleave(2 * s - 1, 0)
                 v_interleave(2 * s - 1, 1)
 
+            if s == EARLY_STEPS:
+                jobs[0][0](*jobs[0][1:])
+                jobs = jobs[1:]
             cuts = [0, 1, 1 if s == LAST else 2, len(jobs)]
             for g in range(GROUPS):
                 if s < TILES:
@@ -316,8 +320,10 @@ def tile_data2vec_head_backward_s9_kernel(tc, x, w_words, w_scales, y, c, v, out
                     tanh(s, g)
                 for job in jobs[cuts[g] : cuts[g + 1]]:
                     job[0](*job[1:])
-                if g < len(turned):
-                    weigh_turned(prev, turned[g])
+                if len(turned) == GROUPS:
+                    weigh_turned(prev, g)
+                elif g == 1 and s > 0:
+                    weigh_turned(prev, turned[0])
                 if s == 0 and g == 0:
                     x_quantise(1)
                 if s == TILES and g > 0:
@@ -328,18 +334,18 @@ def tile_data2vec_head_backward_s9_kernel(tc, x, w_words, w_scales, y, c, v, out
                 v_interleave(0, 1)
             if s + 2 < TILES:
                 x_quantise(s + 2)
+            if rows_groups(s):
+                weigh_rows(s)
             if 0 < s < TILES:
                 for g0, g1 in quantise_pieces(prev):
                     e_quantise(prev, g0, g1)
             if 0 < s <= EARLY_STEPS:
                 v_quantise(2 * s - 2)
                 v_quantise(2 * s - 1)
-            if rows_groups(s):
-                weigh_rows(s)
 
         e_quantise(LAST, GROUPS - 1, GROUPS)
-        product_out(LAST, 0, "e_bank")
-        second_product(LAST, 1, "e_bank")
+        product_out(LAST, 0, "xo_bank")
+        second_product(LAST, 1, "xo_bank")
         for part in range(2):
             cols = slice(part * N // 2, (part + 1) * N // 2)
             res_last = work.tile([P, N // 2], F32, name="res_last", bufs=2, align_bytes=64)

from contextlib import ExitStack

import concourse.mybir as mybir
from concourse.masks import make_identity

M, D, F = 1024, 1024, 1536
FLOPS = 2 * M * D * F * 2

F32 = mybir.dt.float32
BF16 = mybir.dt.bfloat16
I32 = mybir.dt.int32
U32 = mybir.dt.uint32
U8 = mybir.dt.uint8
E4M3 = mybir.dt.float8_e4m3fn_x4
E5M2 = mybir.dt.float8_e5m2_x4
E2M1 = mybir.dt.float4_e2m1fn_x4
ALU = mybir.AluOpType
ACT = mybir.ActivationFunctionType

P = 128
N = 512
SLOTS = 4
TILES = M // P
LAST = TILES - 1
X_PASSES = D // N
GROUPS = F // N
HALVES = D // N
CHUNKS = HALVES * GROUPS

EARLY_STEPS = 3
ROWS_GROUPS = 2
PRODUCTS_PER_STEP = 3


def rows_groups(m):
    return ROWS_GROUPS if EARLY_STEPS <= m < LAST else 0


def quantise_pieces(m):
    return [(g, g + 1) for g in range(GROUPS)] if m == LAST else [(0, 2), (2, 3)]


def x_tiles_of_step(s):
    return [m for m in range(2, TILES) if (2 * m - 3) // 3 == s]


def tile_data2vec_head_backward_s9_kernel(tc, x, w_words, w_scales, y, c, v, out):
    nc = tc.nc
    with ExitStack() as ctx:
        keep = ctx.enter_context(tc.tile_pool(name="keep", bufs=1))
        work = ctx.enter_context(tc.tile_pool(name="work", bufs=2))
        psum = ctx.enter_context(tc.psum_pool(name="psum", bufs=1))
        ctx.enter_context(tc.manual_schedule())

        x_raw = [keep.tile([P, D], BF16, name="x_raw%d" % m, align_bytes=64) for m in range(TILES)]
        y_raw = {m: keep.tile([P, F], BF16, name="y_raw%d" % m, align_bytes=64) for m in range(1, TILES)}
        y_first = keep.tile([P, N], BF16, name="y_first", align_bytes=64)
        y_rest = keep.tile([P, F - N], BF16, name="y_rest", align_bytes=64)
        w_first = keep.tile([P, X_PASSES, 2 * N], U8, name="w_first", align_bytes=64)
        w_rest = keep.tile([P, X_PASSES, 2 * (F - N)], U8, name="w_rest", align_bytes=64)
        w_scale = keep.tile([P, X_PASSES, F], U8, name="w_scale", align_bytes=64)
        v_raw = [keep.tile([P, SLOTS, N], BF16, name="v_raw%d" % i, align_bytes=64) for i in range(CHUNKS)]
        c_col = keep.tile([P, GROUPS, 16], BF16, name="c_col", align_bytes=64)
        c_row = keep.tile([P, ROWS_GROUPS * N], BF16, name="c_row", align_bytes=64)
        ident = keep.tile([P, P], F32, name="ident", align_bytes=64)

        def y_cols(m, g):
            if m > 0:
                return y_raw[m][:, g * N : (g + 1) * N]
            return y_first[:] if g == 0 else y_rest[:, (g - 1) * N : g * N]

        def w_cols(kp, g):
            if g == 0:
                return w_first[:, kp, :]
            return w_rest[:, kp, (g - 1) * 2 * N : g * 2 * N]

        def load_x(m):
            nc.sync.dma_start(out=x_raw[m][:], in_=x[m * P : (m + 1) * P, :])

        def load_y(m):
            nc.sync.dma_start(out=y_raw[m][:], in_=y[m * P : (m + 1) * P, :])

        def load_v(i):
            h, g = divmod(i, GROUPS)
            rows = v[g * N : (g + 1) * N, h * N : (h + 1) * N]
            nc.sync.dma_start(out=v_raw[i][:], in_=rows.rearrange("(p t) n -> p t n", t=SLOTS))

        nc.vector.memset(w_scale[:].rearrange("p g n -> p (g n)").bitcast(I32), 0)
        make_identity(nc, ident[:])

        w_i32 = w_words.bitcast(I32).rearrange("g p n -> p g n")
        s_i32 = w_scales.bitcast(I32).rearrange("g q n -> q g n")
        load_x(0)
        for quad in range(4):
            nc.sync.dma_start(
                out=w_scale[32 * quad : 32 * quad + 4].bitcast(I32), in_=s_i32[4 * quad : 4 * quad + 4]
            )
        nc.sync.dma_start(out=w_first[:].bitcast(I32), in_=w_i32[:, :, 0 : N // 2])
        nc.sync.dma_start(out=y_first[:], in_=y[0:P, 0:N])
        load_x(1)
        nc.sync.dma_start(out=w_rest[:].bitcast(I32), in_=w_i32[:, :, N // 2 : F // 2])
        nc.sync.dma_start(out=y_rest[:], in_=y[0:P, N:F])
        nc.sync.dma_start(out=c_col[:, :, 0:SLOTS], in_=c.rearrange("(g p t) -> p g t", p=P, t=SLOTS))
        for s in range(EARLY_STEPS):
            for m in x_tiles_of_step(s):
                load_x(m)
            load_v(2 * s)
            load_y(s + 1)
            if s + 1 == EARLY_STEPS:
                for m in x_tiles_of_step(EARLY_STEPS):
                    load_x(m)
            load_v(2 * s + 1)
        for m in range(EARLY_STEPS + 1, TILES):
            load_y(m)

        x_bank, x_inter, x_codes, x_scale = {}, {}, {}, {}
        pred, diff, th, e_rows, e_bank, e_inter, e_codes, e_scale = {}, {}, {}, {}, {}, {}, {}, {}
        v_inter, v_codes, v_scale, o_bank = {}, {}, {}, {}

        def x_transpose(m):
            x_bank[m] = psum.tile([P, X_PASSES, 2, P], F32, name="xo_bank", bufs=2)
            words = x_raw[m][:].bitcast(F32)
            for kp in range(X_PASSES):
                for u in range(2):
                    in_words = words[:, kp * N // 2 + u : (kp + 1) * N // 2 : 2]
                    nc.tensor.transpose(x_bank[m][:, kp, u, :], in_words, ident[:])

        def x_copy(m):
            x_inter[m] = work.tile([P, D], BF16, name="x_inter", bufs=TILES, align_bytes=64)
            nc.scalar.copy(
                out=x_inter[m][:].bitcast(F32).rearrange("p (g r u) -> p g r u", g=X_PASSES, u=2),
                in_=x_bank[m][:].rearrange("p g u r -> p g r u"),
            )

        def x_quantise(m):
            x_codes[m] = work.tile([P, D // SLOTS], U32, name="x_codes", bufs=3, align_bytes=64)
            x_scale[m] = work.tile([P, D // SLOTS], U8, name="x_scale", bufs=3, align_bytes=64)
            nc.vector.quantize_mx(out=x_codes[m][:].bitcast(E4M3), scales=x_scale[m][:], in_=x_inter[m][:])

        def c_spread():
            words = c_col[:].bitcast(F32)
            bank = psum.tile([P, ROWS_GROUPS, 2, P], F32, name="xo_bank", bufs=2)
            for g in range(ROWS_GROUPS):
                for u in range(2):
                    nc.tensor.transpose(bank[:, g, u, :], words[:, g, u : u + 1].to_broadcast([P, P]), ident[:])
            nc.scalar.copy(out=c_row[:].bitcast(F32), in_=bank[:].rearrange("p g u r -> p (g u r)"))

        def first_product(m, g):
            pred[m, g] = psum.tile([P, N], F32, name="pred", bufs=3)
            for kp in range(X_PASSES):
                nc.tensor.matmul_mx(
                    out=pred[m, g][:],
                    lhsT=x_codes[m][:, kp * P : (kp + 1) * P].bitcast(E4M3),
                    lhsT_scale=x_scale[m][:, kp * P : (kp + 1) * P],
                    rhs=w_cols(kp, g).bitcast(E2M1),
                    rhs_scale=w_scale[:, kp, g * N : (g + 1) * N],
                    start=(kp == 0),
                    stop=(kp == X_PASSES - 1),
                )

        def subtract(m, g):
            runs, pair = (2, 2) if g < rows_groups(m) else (SLOTS, 1)
            diff[m, g] = work.tile([P, N], F32, name="diff", bufs=3, align_bytes=64)
            nc.vector.tensor_tensor(
                out=diff[m, g][:].rearrange("p (u q e) -> p u q e", u=runs, e=pair),
                in0=pred[m, g][:].rearrange("p (q u e) -> p u q e", u=runs, e=pair),
                in1=y_cols(m, g).rearrange("p (q u e) -> p u q e", u=runs, e=pair),
                op=ALU.subtract,
            )

        def tanh(m, g):
            if g == 0:
                th[m] = work.tile([P, F], F32, name="th", bufs=2, align_bytes=64)
            nc.scalar.activation(out=th[m][:, g * N : (g + 1) * N], in_=diff[m, g][:], func=ACT.Tanh)

        def th_transpose(m, g):
            e_bank[m, g] = psum.tile([P, SLOTS, P], F32, name="pred" if m == LAST else "e_bank", bufs=3)
            for t in range(SLOTS):
                first = g * N + t * P
                nc.tensor.transpose(e_bank[m, g][:, t, :], th[m][:, first : first + P], ident[:])

        def piece_of(m, g):
            return [(g0, g1) for g0, g1 in quantise_pieces(m) if g0 <= g < g1][0]

        def weigh_turned(m, g):
            g0, g1 = piece_of(m, g)
            if g == g0:
                e_inter[m, g0] = work.tile([P, (g1 - g0) * N], BF16, name="e_inter%d" % g0, bufs=2, align_bytes=64)
            nc.vector.tensor_tensor(
                out=e_inter[m, g0][:, (g - g0) * N : (g - g0 + 1) * N].rearrange("p (r t) -> p r t", t=SLOTS),
                in0=e_bank[m, g][:].rearrange("p t r -> p r t"),
                in1=c_col[:, g : g + 1, 0:SLOTS].to_broadcast([P, P, SLOTS]),
                op=ALU.mult,
            )

        def weigh_rows(m):
            e_rows[m] = work.tile([P, ROWS_GROUPS * N], BF16, name="e_rows", bufs=2, align_bytes=64)
            nc.vector.tensor_tensor(out=e_rows[m][:], in0=th[m][:, 0 : ROWS_GROUPS * N], in1=c_row[:], op=ALU.mult)

        def rows_transpose(m):
            e_bank[m, 0] = psum.tile([P, ROWS_GROUPS, 2, P], F32, name="e_bank", bufs=3)
            words = e_rows[m][:].bitcast(F32).rearrange("p (g u q) -> p g u q", g=ROWS_GROUPS, u=2)
            for g in range(ROWS_GROUPS):
                for u in range(2):
                    nc.tensor.transpose(e_bank[m, 0][:, g, u, :], words[:, g, u, :], ident[:])

        def rows_copy(m):
            e_inter[m, 0] = work.tile([P, ROWS_GROUPS * N], BF16, name="e_inter0", bufs=2, align_bytes=64)
            nc.scalar.copy(
                out=e_inter[m, 0][:].bitcast(F32).rearrange("p (g r u) -> p g r u", r=P, u=2),
                in_=e_bank[m, 0][:].rearrange("p g u r -> p g r u"),
            )

        def e_quantise(m, g0, g1):
            e_codes[m, g0] = keep.tile([P, (g1 - g0) * P], U32, name="e_codes%d_%d" % (m, g0), align_bytes=64)
            e_scale[m, g0] = keep.tile([P, (g1 - g0) * P], U8, name="e_scale%d_%d" % (m, g0), align_bytes=64)
            nc.vector.quantize_mx(out=e_codes[m, g0][:].bitcast(E5M2), scales=e_scale[m, g0][:], in_=e_inter[m, g0][:])

        def v_interleave(i, part):
            cols = slice(part * N // 2, (part + 1) * N // 2)
            if i % 2 == 1:
                if part == 0:
                    v_inter[i] = work.tile([P, N, SLOTS], BF16, name="v_inter_gpsimd", bufs=1, align_bytes=64)
                src = v_raw[i][:, :, cols].rearrange("p t n -> p n t")
                nc.gpsimd.tensor_scalar(
                    out=v_inter[i][:, cols, :], in0=src, scalar1=1.0, scalar2=0.0, op0=ALU.mult, op1=ALU.add
                )
                return
            if part == 0:
                v_inter[i] = work.tile([P, N, SLOTS], BF16, name="v_inter", bufs=3, align_bytes=64)
            dst = v_inter[i][:, cols, :].rearrange("p (a b) t -> p a t b", b=4)
            src = v_raw[i][:, :, cols].rearrange("p t (a b) -> p a t b", b=4)
            if i == 0:
                nc.vector.tensor_copy(out=dst, in_=src)
            else:
                nc.scalar.copy(out=dst, in_=src)

        def v_quantise(i):
            v_codes[i] = keep.tile([P, N], U32, name="v_codes%d" % i, align_bytes=64)
            v_scale[i] = keep.tile([P, N], U8, name="v_scale%d" % i, align_bytes=64)
            nc.vector.quantize_mx(
                out=v_codes[i][:].bitcast(E4M3), scales=v_scale[i][:], in_=v_inter[i][:].rearrange("p n t -> p (n t)")
            )

        def second_product(m, h, tag):
            o_bank[m, h] = psum.tile([P, N], F32, name=tag, bufs=3 if tag == "e_bank" else 2)
            for g in range(GROUPS):
                g0 = piece_of(m, g)[0]
                cols = slice((g - g0) * P, (g - g0 + 1) * P)
                nc.tensor.matmul_mx(
                    out=o_bank[m, h][:],
                    lhsT=e_codes[m, g0][:, cols].bitcast(E5M2),
                    lhsT_scale=e_scale[m, g0][:, cols],
                    rhs=v_codes[h * GROUPS + g][:].bitcast(E4M3),
                    rhs_scale=v_scale[h * GROUPS + g][:],
                    start=(g == 0),
                    stop=(g == GROUPS - 1),
                )

        def product_out(m, h, tag):
            second_product(m, h, tag)
            res = work.tile([P, N], F32, name="res", bufs=4, align_bytes=64)
            nc.scalar.copy(out=res[:], in_=o_bank[m, h][:])
            nc.sync.dma_start(out=out[m * P : (m + 1) * P, h * N : (h + 1) * N], in_=res[:])

        x_transpose(0)
        x_copy(0)
        x_quantise(0)
        first_product(0, 0)
        x_transpose(1)
        x_copy(1)
        for g in range(1, GROUPS):
            first_product(0, g)

        waiting = [(m, h) for m in range(LAST) for h in range(HALVES)]
        for s in range(TILES + 1):
            prev = s - 1
            turned = range(rows_groups(prev), GROUPS) if s > 0 else range(0)
            ready = [
                (m, h) for m, h in waiting if (m, 0) in e_codes and (h + 1) * GROUPS - 1 in v_codes
            ][:PRODUCTS_PER_STEP]
            for product in ready:
                waiting.remove(product)

            if EARLY_STEPS < s < TILES:
                for g in range(GROUPS):
                    first_product(s, g)
            for g in turned:
                if s <= EARLY_STEPS:
                    first_product(s, g)
                th_transpose(prev, g)
                if s == EARLY_STEPS and g < len(x_tiles_of_step(s)):
                    x_transpose(x_tiles_of_step(s)[g])
            jobs = []
            if rows_groups(prev):
                rows_transpose(prev)
                jobs.append((rows_copy, prev))
            for m in x_tiles_of_step(s):
                if s < EARLY_STEPS:
                    x_transpose(m)
                jobs.append((x_copy, m))
            if s == 0:
                jobs.append((c_spread,))
            for j, (m, h) in enumerate(ready):
                spare = s == TILES or (j == PRODUCTS_PER_STEP - 1 and rows_groups(prev) > 0)
                jobs.append((product_out, m, h, "e_bank" if spare else "xo_bank"))
            if 0 < s < EARLY_STEPS:
                jobs.extend([(v_interleave, 2 * s, 0), (v_interleave, 2 * s, 1)])
            if 0 < s <= EARLY_STEPS:
                v_interleave(2 * s - 1, 0)
                v_interleave(2 * s - 1, 1)

            if s == EARLY_STEPS:
                jobs[0][0](*jobs[0][1:])
                jobs = jobs[1:]
            cuts = [0, 1, 1 if s == LAST else 2, len(jobs)]
            for g in range(GROUPS):
                if s < TILES:
                    subtract(s, g)
                    tanh(s, g)
                for job in jobs[cuts[g] : cuts[g + 1]]:
                    job[0](*job[1:])
                if len(turned) == GROUPS:
                    weigh_turned(prev, g)
                elif g == 1 and s > 0:
                    weigh_turned(prev, turned[0])
                if s == 0 and g == 0:
                    x_quantise(1)
                if s == TILES and g > 0:
                    e_quantise(LAST, g - 1, g)

            if s == 0:
                v_interleave(0, 0)
                v_interleave(0, 1)
            if s + 2 < TILES:
                x_quantise(s + 2)
            if rows_groups(s):
                weigh_rows(s)
            if 0 < s < TILES:
                for g0, g1 in quantise_pieces(prev):
                    e_quantise(prev, g0, g1)
            if 0 < s <= EARLY_STEPS:
                v_quantise(2 * s - 2)
                v_quantise(2 * s - 1)

        e_quantise(LAST, GROUPS - 1, GROUPS)
        product_out(LAST, 0, "xo_bank")
        second_product(LAST, 1, "xo_bank")
        for part in range(2):
            cols = slice(part * N // 2, (part + 1) * N // 2)
            res_last = work.tile([P, N // 2], F32, name="res_last", bufs=2, align_bytes=64)
            nc.vector.tensor_copy(out=res_last[:], in_=o_bank[LAST, 1][:, cols])
            nc.sync.dma_start(out=out[LAST * P :, N + cols.start : N + cols.stop], in_=res_last[:])
